import numpy as np
import ml_dtypes


def mxq(x, axis, fmt="e4m3"):
    dtype, down = {"e4m3": (ml_dtypes.float8_e4m3fn, 7), "e5m2": (ml_dtypes.float8_e5m2, 14)}[fmt]
    v = np.moveaxis(np.asarray(x, np.float32).astype(ml_dtypes.bfloat16).astype(np.float64), axis, -1)
    blocks = v.reshape(v.shape[:-1] + (-1, 32))
    amax = np.abs(blocks).max(-1, keepdims=True)
    byte = np.maximum(np.where(amax > 0, np.frexp(amax)[1] - 1 + 127, 0) - down, 1)
    scale = np.exp2(byte - 127.0)
    codes = (blocks / scale).astype(np.float32).astype(dtype).astype(np.float64)
    return np.moveaxis((codes * scale).reshape(v.shape), -1, axis)


WIDE = False


def mx_kscale(k):
    if not WIDE:
        return np.ones(k)
    levels = np.array([10, -10, 5, -5, 0])
    if k % 512:
        return np.exp2(np.random.permutation(np.resize(levels, k // 32))).repeat(32)
    a = np.empty((k // 512, 16))
    for p in range(k // 512):
        a[p, :8] = np.random.permutation(np.resize(levels, 8))
        for g in range(8):
            far = levels[np.abs(levels - a[p, g]) >= 10]
            a[p, g + 8] = far[np.random.randint(len(far))]
    return np.exp2(a.ravel()).repeat(32)


def f64(x):
    return np.asarray(x).astype(np.float64)


def striped8(idx):
    return np.asarray(idx).reshape(8, -1, 16).transpose(0, 2, 1).reshape(128, -1).astype(np.uint16)


def unstriped8(offs):
    return offs.reshape(8, 16, -1).transpose(0, 2, 1).reshape(8, -1).astype(np.int64)


def pick8(x, idx, run):
    r = np.arange(len(x))
    return x[r[:, None], idx[r % (8 * run) // run]]


E2M1 = np.array([0.0, 0.5, 1.0, 1.5, 2.0, 3.0, 4.0, 6.0, -0.0, -0.5, -1.0, -1.5, -2.0, -3.0, -4.0, -6.0])


def pack_weight(w, fmt):
    k, n = w.shape
    w = f64(np.asarray(w, np.float32).astype(ml_dtypes.bfloat16)).reshape(k // 32, 32, n)
    amax = np.abs(w).max(1)
    if fmt == "e4m3":
        byte = np.frexp(amax)[1] - 1 + 127 - 7
    else:
        mant, ex = np.frexp(amax / 6.0)
        byte = np.where(mant > 0.5, ex, ex - 1) + 127
    byte = np.clip(np.where(amax > 0, byte, 1), 1, 254)
    scaled = (w * np.exp2(127.0 - byte)[:, None, :]).reshape(k, n).astype(np.float32)
    by_word = np.ascontiguousarray(scaled.reshape(k // 512, 128, 4, n).transpose(0, 1, 3, 2))
    if fmt == "e4m3":
        words = by_word.astype(ml_dtypes.float8_e4m3fn).view(np.uint8)
    else:
        c = by_word.astype(ml_dtypes.float4_e2m1fn).view(np.uint8) & 0xF
        words = (c[..., 0::2] | (c[..., 1::2] << 4)).reshape(k // 512, 128, 2 * n)
    return np.ascontiguousarray(words), np.ascontiguousarray(byte.astype(np.uint8).reshape(k // 512, 16, n))


def unpack_weight(words, scales, fmt):
    g, _, n = scales.shape
    words = np.ascontiguousarray(words).reshape(g, 128, n, -1)
    if fmt == "e4m3":
        vals = words.view(ml_dtypes.float8_e4m3fn).astype(np.float64)
    else:
        nib = np.empty((g, 128, n, 4), np.uint8)
        nib[..., 0::2] = words & 0xF
        nib[..., 1::2] = words >> 4
        vals = E2M1[nib]
    vals = vals * np.repeat(np.exp2(scales.astype(np.float64) - 127.0), 8, axis=1)[..., None]
    return vals.transpose(0, 1, 3, 2).reshape(g * 512, n)


D, E, T, Q, I = 512, 512, 1024, 128, 512


def setup_inputs():
    n = np.random.standard_normal
    idx = np.stack([np.random.permutation(T)[:I] for _ in range(8)])
    idx2 = np.stack([np.random.permutation(T)[:I] for _ in range(8)])
    fd = mx_kscale(D)
    fe = mx_kscale(E)
    keysp = pack_weight(n((D, T)) / fd[:, None], "e4m3")
    return {
        "query": (n((D, Q)) * 0.7 / np.sqrt(D) * fd[:, None]).astype(np.float32),
        "keys_words": keysp[0],
        "keys_scales": keysp[1],
        "gout": (n((E, Q)) * 1 / np.sqrt(E) * fe[:, None]).astype(np.float32),
        "vals": (n((E, T)) / fe[:, None]).astype(np.float32),
        "dquery": (n((D, Q)) * 1.0 / np.sqrt(D) * fd[:, None]).astype(np.float32),
        "base": (0.5 * n((Q, T))).astype(np.float32),
        "offs": striped8(idx),
        "offs2": striped8(idx2),
    }


def reference(query, keys_words, keys_scales, gout, vals, dquery, base, offs, offs2):
    idx = unstriped8(offs)
    idx2 = unstriped8(offs2)
    keysu = unpack_weight(keys_words, keys_scales, "e4m3")
    queryq = mxq(f64(query), 0, "e4m3")
    a = queryq.T @ keysu
    dqueryq = mxq(f64(dquery), 0, "e4m3")
    ta = dqueryq.T @ keysu
    s = pick8(a, idx, 16) * pick8(a, idx2, 16) + (pick8(a, idx, 16) + pick8(a, idx2, 16)) * 0.5
    p = np.exp(s - np.max(s, axis=1, keepdims=True))
    z = np.sum(p, axis=1, keepdims=True)
    goutq = mxq(f64(gout), 0, "e4m3")
    valsq = mxq(f64(vals), 0, "e4m3")
    c0 = goutq.T @ valsq
    dw = pick8(c0, idx, 16)
    dz = np.sum(dw * p / np.square(z) * (-1.0), axis=1, keepdims=True)
    dp = dw / z + dz
    ds = dp * p
    xs = pick8(ta, idx, 16) * pick8(a, idx2, 16) + pick8(ta, idx2, 16) * pick8(a, idx, 16) + (pick8(ta, idx, 16) + pick8(ta, idx2, 16)) * 0.5
    xp = xs * p
    xz = np.sum(xp, axis=1, keepdims=True)
    xdz = np.sum((xp * dw - xz * z * 2.0 * dw * p / np.square(z)) / np.square(z) * (-1.0), axis=1, keepdims=True)
    xdp = xz * dw / np.square(z) * (-1.0) + xdz
    xds = xdp * p + xp * dp
    xe1 = xds * pick8(a, idx2, 16) + pick8(ta, idx2, 16) * ds
    xs1 = np.zeros((Q, T))
    xs1[np.arange(Q)[:, None], idx[np.arange(Q) % 128 // 16]] = xe1
    xe2 = xds * 0.5
    xs2 = np.zeros((Q, T))
    xs2[np.arange(Q)[:, None], idx[np.arange(Q) % 128 // 16]] = xe2
    xe3 = xds * pick8(a, idx, 16) + pick8(ta, idx, 16) * ds
    xs3 = np.zeros((Q, T))
    xs3[np.arange(Q)[:, None], idx2[np.arange(Q) % 128 // 16]] = xe3
    xe4 = xds * 0.5
    xs4 = np.zeros((Q, T))
    xs4[np.arange(Q)[:, None], idx2[np.arange(Q) % 128 // 16]] = xe4
    xda = xs1 + xs2 + xs3 + xs4
    y = xda * 512.0 + f64(base)
    return y

@@ -1,0 +1,186 @@
+from contextlib import ExitStack
+
+import concourse.mybir as mybir
+from concourse.masks import make_identity
+
+D, E, T, Q, I = 512, 512, 1024, 128, 512
+FLOPS = 2 * Q * T * (2 * D + E)
+
+F32 = mybir.dt.float32
+BF16 = mybir.dt.bfloat16
+I32 = mybir.dt.int32
+U32 = mybir.dt.uint32
+U16 = mybir.dt.uint16
+U8 = mybir.dt.uint8
+FP8X4 = mybir.dt.float8_e4m3fn_x4
+ALU = mybir.AluOpType
+ACT = mybir.ActivationFunctionType
+AX = mybir.AxisListType
+
+P = 128
+PACK = 4
+BANK = 512
+PIECE = 256
+
+
+def interleave(copy, pool, raw, width, name):
+    grouped = pool.tile([P, width, PACK], BF16, align_bytes=64, name=name)
+    copy(out=grouped[:].rearrange("p (c i) j -> p c j i", i=4), in_=raw[:].rearrange("p j (c i) -> p c j i", i=4))
+    return grouped
+
+
+def quantize(nc, pool, grouped, width, name):
+    codes = pool.tile([P, width], U32, align_bytes=64, name=name + "_codes")
+    scales = pool.tile([P, width], U8, align_bytes=64, name=name + "_scales")
+    nc.vector.quantize_mx(out=codes[:].bitcast(FP8X4), scales=scales[:], in_=grouped[:].rearrange("p w j -> p (w j)"))
+    return codes, scales
+
+
+def product(nc, bank, rows, codes, scales):
+    nc.tensor.matmul_mx(out=bank, lhsT=rows[0][:].bitcast(FP8X4), lhsT_scale=rows[1][:],
+                        rhs=codes.bitcast(FP8X4), rhs_scale=scales, start=True, stop=True)
+
+
+def tile_attend_hvproductpairs_heads_kernel(tc, query, keys_words, keys_scales, gout, vals, dquery, base, offs, offs2, out):
+    nc = tc.nc
+    with ExitStack() as ctx:
+        lists = ctx.enter_context(tc.tile_pool(name="lists", bufs=1))
+        sb = ctx.enter_context(tc.tile_pool(name="sb", bufs=1))
+        psum = ctx.enter_context(tc.psum_pool(name="psum", bufs=1))
+
+        def load_rows(src, width, name):
+            raw = sb.tile([P, PACK, width], F32, name=name)
+            nc.sync.dma_start(out=raw[:], in_=src.rearrange("(p j) w -> p j w", j=PACK))
+            return raw
+
+        key_scales = sb.tile([P, T], U8, align_bytes=64)
+        nc.vector.memset(key_scales[:].bitcast(I32), 0)
+        zero = sb.tile([P, 1], F32)
+        nc.vector.memset(zero[:], 0.0)
+        placed1 = sb.tile([P, T], F32)
+        placed2 = sb.tile([P, T], F32)
+        nc.vector.memset(placed1[:], 0.0)
+        nc.vector.memset(placed2[:], 0.0)
+
+        query_raw = load_rows(query, Q, "query_raw")
+        for quad in range(4):
+            nc.scalar.dma_start(out=key_scales[32 * quad : 32 * quad + 4, :].bitcast(I32),
+                                in_=keys_scales[0, 4 * quad : 4 * quad + 4, :].bitcast(I32))
+        key_bytes = keys_words[0].rearrange("p n r -> p (n r)")
+        key_words = []
+        for h in range(T // BANK):
+            words = sb.tile([P, BANK], U32, align_bytes=64, name=f"key_words{h}")
+            nc.sync.dma_start(out=words[:].bitcast(I32), in_=key_bytes[:, PACK * BANK * h : PACK * BANK * (h + 1)].bitcast(I32))
+            key_words.append(words)
+        dquery_raw = load_rows(dquery, Q, "dquery_raw")
+        list1 = lists.tile([P, I // 16], U16)
+        list2 = lists.tile([P, I // 16], U16)
+        nc.sync.dma_start(list1[:], offs)
+        nc.sync.dma_start(list2[:], offs2)
+        gout_raw = load_rows(gout, Q, "gout_raw")
+        vals_raw = [load_rows(vals[:, PIECE * c : PIECE * (c + 1)], PIECE, f"vals_raw{c}") for c in range(T // PIECE)]
+        base_sb = sb.tile([P, T], F32)
+        nc.sync.dma_start(out=base_sb[:], in_=base)
+
+        warm = sb.tile([P, 1], F32)
+        nc.scalar.activation(out=warm[:], in_=zero[:], func=ACT.Exp)
+        identity = sb.tile([P, P], F32)
+        make_identity(nc, identity[:])
+
+        query_q = quantize(nc, sb, interleave(nc.vector.tensor_copy, sb, query_raw, Q, "query_bf"), Q, "query")
+        a = sb.tile([P, T], F32)
+        for c in range(T // PIECE):
+            bank = psum.tile([P, PIECE], F32, name=f"bank{c}")
+            h, lo = divmod(PIECE * c, BANK)
+            product(nc, bank[:], query_q, key_words[h][:, lo : lo + PIECE], key_scales[:, PIECE * c : PIECE * (c + 1)])
+            copy = nc.scalar.copy if c % 2 == 0 else nc.vector.tensor_copy
+            copy(out=a[:, PIECE * c : PIECE * (c + 1)], in_=bank[:])
+
+        dquery_q = quantize(nc, sb, interleave(nc.vector.tensor_copy, sb, dquery_raw, Q, "dquery_bf"), Q, "dquery")
+        ta = sb.tile([P, T], F32)
+        for h in range(T // BANK):
+            bank = psum.tile([P, BANK], F32, name=f"wide{h}")
+            product(nc, bank[:], dquery_q, key_words[h][:], key_scales[:, BANK * h : BANK * (h + 1)])
+            nc.scalar.copy(out=ta[:, BANK * h : BANK * (h + 1)], in_=bank[:])
+
+        def slots(name):
+            return sb.tile([P, I], F32, name=name)
+
+        def column(name):
+            return sb.tile([P, 1], F32, name=name)
+
+        b1, b2, t1, t2, w = slots("b1"), slots("b2"), slots("t1"), slots("t2"), slots("w")
+        nc.vector.tensor_scalar(b1[:], a[:].indirect(list1[:]), 1.0, 0.5, ALU.mult, ALU.add)
+        nc.vector.tensor_scalar(b2[:], a[:].indirect(list2[:]), 1.0, 0.5, ALU.mult, ALU.add)
+
+        gout_bf = interleave(nc.scalar.copy, sb, gout_raw, Q, "gout_bf")
+        vals_bf = [interleave(nc.scalar.copy, sb, vals_raw[c], PIECE, f"vals_bf{c}") for c in range(2)]
+
+        nc.vector.tensor_copy(t1[:], ta[:].indirect(list1[:]))
+        s, p, pn = slots("s"), slots("p"), slots("pn")
+        nc.vector.tensor_tensor(s[:], b1[:], b2[:], ALU.mult)
+        gout_q = quantize(nc, sb, gout_bf, Q, "gout")
+        neg_max, z, rz = column("neg_max"), column("z"), column("rz")
+        nc.vector.tensor_reduce(neg_max[:], s[:], AX.X, ALU.max, negate=True)
+        nc.scalar.activation(out=p[:], in_=s[:], func=ACT.Exp, bias=neg_max[:], scale=1.0, accum_out=z[:])
+        vals_bf.extend(interleave(nc.scalar.copy, sb, vals_raw[c], PIECE, f"vals_bf{c}") for c in range(2, 4))
+        nc.vector.tensor_copy(t2[:], ta[:].indirect(list2[:]))
+
+        c0 = sb.tile([P, T], F32)
+
+        def values_piece(c):
+            codes, scales = quantize(nc, sb, vals_bf[c], PIECE, f"vals{c}")
+            bank = psum.tile([P, PIECE], F32, name=f"bank{c}")
+            product(nc, bank[:], gout_q, codes[:], scales[:])
+            nc.scalar.copy(out=c0[:, PIECE * c : PIECE * (c + 1)], in_=bank[:])
+
+        values_piece(0)
+        values_piece(1)
+        nc.vector.reciprocal(rz[:], z[:])
+        x1, x2, xs = slots("x1"), slots("x2"), slots("xs")
+        nc.vector.tensor_tensor(x1[:], t1[:], b2[:], ALU.mult)
+        values_piece(2)
+        nc.vector.tensor_tensor(x2[:], t2[:], b1[:], ALU.mult)
+        values_piece(3)
+        nc.scalar.activation(out=pn[:], in_=p[:], func=ACT.Copy, scale=rz[:])
+        nc.vector.tensor_tensor(xs[:], x1[:], x2[:], ALU.add)
+
+        blocks = BANK // P
+        turned = [psum.tile([P, BANK], F32, name=f"turned{h}") for h in range(T // BANK)]
+
+        def turn_add(src, first, last):
+            for h in range(T // BANK):
+                for b in range(blocks):
+                    col = BANK * h + P * b
+                    nc.tensor.matmul(turned[h][:, P * b : P * (b + 1)], lhsT=src[:, col : col + P], rhs=identity[:],
+                                     is_transpose=True, start=first and b == 0, stop=last and b == blocks - 1)
+
+        turn_add(base_sb, True, False)
+
+        nc.vector.tensor_scalar(w[:], c0[:].indirect(list1[:]), 512.0, 0.0, ALU.mult, ALU.add)
+        u, m, c = column("u"), column("m"), column("c")
+        xp, wp, ds, r, nx = slots("xp"), slots("wp"), slots("ds"), slots("r"), slots("nx")
+        nc.vector.scalar_tensor_tensor(xp[:], xs[:], rz[:], p[:], ALU.mult, ALU.mult, accum_out=u[:])
+        nc.vector.scalar_tensor_tensor(wp[:], w[:], 1.0, pn[:], ALU.mult, ALU.mult, accum_out=m[:])
+        nc.vector.scalar_tensor_tensor(ds[:], w[:], m[:], pn[:], ALU.subtract, ALU.mult)
+        nc.vector.scalar_tensor_tensor(r[:], xs[:], u[:], ds[:], ALU.subtract, ALU.mult, accum_out=c[:])
+        g1, g2, f1, f2 = slots("g1"), slots("g2"), slots("f1"), slots("f2")
+        nc.vector.tensor_tensor(g1[:], t2[:], ds[:], ALU.mult)
+        nc.vector.scalar_tensor_tensor(nx[:], pn[:], c[:], r[:], ALU.mult, ALU.subtract)
+        nc.vector.tensor_tensor(g2[:], t1[:], ds[:], ALU.mult)
+        nc.vector.scalar_tensor_tensor(f1[:], nx[:], -1.0, b2[:], ALU.mult, ALU.mult)
+        nc.vector.scalar_tensor_tensor(f2[:], nx[:], -1.0, b1[:], ALU.mult, ALU.mult)
+        nc.vector.tensor_tensor(placed1[:].indirect(list1[:]), f1[:], g1[:], ALU.add)
+        nc.vector.tensor_tensor(placed2[:].indirect(list2[:]), f2[:], g2[:], ALU.add)
+
+        turn_add(placed1, False, True)
+        result = sb.tile([P, T], F32)
+        for h in range(T // BANK):
+            turned_sb = sb.tile([P, BANK], F32, name=f"turned_sb{h}")
+            nc.scalar.copy(out=turned_sb[:], in_=turned[h][:])
+            back = psum.tile([P, BANK], F32, name=f"wide{h}")
+            for b in range(blocks):
+                nc.tensor.transpose(back[:, P * b : P * (b + 1)], turned_sb[:, P * b : P * (b + 1)], identity[:])
+            cols = slice(BANK * h, BANK * (h + 1))
+            nc.vector.tensor_tensor(result[:, cols], back[:], placed2[:, cols], ALU.add)
+            nc.sync.dma_start(out=out[:, cols], in_=result[:, cols])

@@ -23,8 +23,8 @@ BANK = 512
 PIECE = 256
 
 
-def interleave(copy, pool, raw, width, name):
-    grouped = pool.tile([P, width, PACK], BF16, align_bytes=64, name=name)
+def interleave(copy, pool, raw, width, name, offset=None):
+    grouped = pool.tile([P, width, PACK], BF16, align_bytes=64, name=name, offset=offset)
     copy(out=grouped[:].rearrange("p (c i) j -> p c j i", i=4), in_=raw[:].rearrange("p j (c i) -> p c j i", i=4))
     return grouped
 
@@ -46,15 +46,15 @@ def tile_attend_hvproductpairs_heads_kernel(tc, query, keys_words, keys_scales, 
     with ExitStack() as ctx:
         lists = ctx.enter_context(tc.tile_pool(name="lists", bufs=1))
         sb = ctx.enter_context(tc.tile_pool(name="sb", bufs=1))
+        reuse = ctx.enter_context(tc.tile_pool(name="reuse", bufs=1))
         psum = ctx.enter_context(tc.psum_pool(name="psum", bufs=1))
 
-        def load_rows(src, width, name):
-            raw = sb.tile([P, PACK, width], F32, name=name)
+        def load_rows(src, width, name, pool=sb, offset=None):
+            raw = pool.tile([P, PACK, width], F32, name=name, offset=offset)
             nc.sync.dma_start(out=raw[:], in_=src.rearrange("(p j) w -> p j w", j=PACK))
             return raw
 
         key_scales = sb.tile([P, T], U8, align_bytes=64)
-        nc.vector.memset(key_scales[:].bitcast(I32), 0)
         zero = sb.tile([P, 1], F32)
         nc.vector.memset(zero[:], 0.0)
         placed1 = sb.tile([P, T], F32)
@@ -78,7 +78,8 @@ def tile_attend_hvproductpairs_heads_kernel(tc, query, keys_words, keys_scales, 
         nc.sync.dma_start(list1[:], offs)
         nc.sync.dma_start(list2[:], offs2)
         gout_raw = load_rows(gout, Q, "gout_raw")
-        vals_raw = [load_rows(vals[:, PIECE * c : PIECE * (c + 1)], PIECE, f"vals_raw{c}") for c in range(T // PIECE)]
+        vals_raw = [load_rows(vals[:, PIECE * c : PIECE * (c + 1)], PIECE, f"vals_raw{c}") for c in range(T // PIECE - 1)]
+        vals_raw.append(load_rows(vals[:, T - PIECE :], PIECE, "vals_raw3", reuse, 0))
         base_sb = sb.tile([P, T], F32)
         nc.sync.dma_start(out=base_sb[:], in_=base)
 
@@ -93,57 +94,67 @@ def tile_attend_hvproductpairs_heads_kernel(tc, query, keys_words, keys_scales, 
             bank = psum.tile([P, PIECE], F32, name=f"bank{c}")
             h, lo = divmod(PIECE * c, BANK)
             product(nc, bank[:], query_q, key_words[h][:, lo : lo + PIECE], key_scales[:, PIECE * c : PIECE * (c + 1)])
-            copy = nc.scalar.copy if c % 2 == 0 else nc.vector.tensor_copy
-            copy(out=a[:, PIECE * c : PIECE * (c + 1)], in_=bank[:])
+            nc.vector.tensor_copy(out=a[:, PIECE * c : PIECE * (c + 1)], in_=bank[:])
 
-        dquery_q = quantize(nc, sb, interleave(nc.vector.tensor_copy, sb, dquery_raw, Q, "dquery_bf"), Q, "dquery")
+        dquery_q = quantize(nc, sb, interleave(nc.scalar.copy, sb, dquery_raw, Q, "dquery_bf"), Q, "dquery")
         ta = sb.tile([P, T], F32)
         for h in range(T // BANK):
             bank = psum.tile([P, BANK], F32, name=f"wide{h}")
             product(nc, bank[:], dquery_q, key_words[h][:], key_scales[:, BANK * h : BANK * (h + 1)])
             nc.scalar.copy(out=ta[:, BANK * h : BANK * (h + 1)], in_=bank[:])
 
-        def slots(name):
-            return sb.tile([P, I], F32, name=name)
+        def slots(name, tag=""):
+            return sb.tile([P, I], F32, name=name, tag=tag, align_bytes=64)
 
         def column(name):
             return sb.tile([P, 1], F32, name=name)
 
-        b1, b2, t1, t2, w = slots("b1"), slots("b2"), slots("t1"), slots("t2"), slots("w")
+        b1, b2 = slots("b1"), slots("b2")
         nc.vector.tensor_scalar(b1[:], a[:].indirect(list1[:]), 1.0, 0.5, ALU.mult, ALU.add)
         nc.vector.tensor_scalar(b2[:], a[:].indirect(list2[:]), 1.0, 0.5, ALU.mult, ALU.add)
 
+        def slots_at(name, offset):
+            return reuse.tile([P, I], F32, name=name, offset=offset)
+
+        KB = 1024
         gout_bf = interleave(nc.scalar.copy, sb, gout_raw, Q, "gout_bf")
-        vals_bf = [interleave(nc.scalar.copy, sb, vals_raw[c], PIECE, f"vals_bf{c}") for c in range(2)]
-
-        nc.vector.tensor_copy(t1[:], ta[:].indirect(list1[:]))
-        s, p, pn = slots("s"), slots("p"), slots("pn")
-        nc.vector.tensor_tensor(s[:], b1[:], b2[:], ALU.mult)
+        first_bf = sb.tile([P, PIECE, PACK], BF16, align_bytes=64)
+        nc.gpsimd.tensor_scalar(first_bf[:], vals_raw[0][:].rearrange("p j w -> p w j"), 1.0, 0.0, ALU.mult, ALU.add)
+        vals_bf = [
+            first_bf,
+            interleave(nc.scalar.copy, sb, vals_raw[1], PIECE, "vals_bf1"),
+            interleave(nc.scalar.copy, sb, vals_raw[2], PIECE, "vals_bf2"),
+            interleave(nc.scalar.copy, reuse, vals_raw[3], PIECE, "vals_bf3", 11 * KB),
+        ]
         gout_q = quantize(nc, sb, gout_bf, Q, "gout")
-        neg_max, z, rz = column("neg_max"), column("z"), column("rz")
-        nc.vector.tensor_reduce(neg_max[:], s[:], AX.X, ALU.max, negate=True)
-        nc.scalar.activation(out=p[:], in_=s[:], func=ACT.Exp, bias=neg_max[:], scale=1.0, accum_out=z[:])
-        vals_bf.extend(interleave(nc.scalar.copy, sb, vals_raw[c], PIECE, f"vals_bf{c}") for c in range(2, 4))
-        nc.vector.tensor_copy(t2[:], ta[:].indirect(list2[:]))
-
-        c0 = sb.tile([P, T], F32)
+        c0_banks = [psum.tile([P, BANK], F32, name=f"bank{h}") for h in range(T // BANK)]
 
         def values_piece(c):
             codes, scales = quantize(nc, sb, vals_bf[c], PIECE, f"vals{c}")
-            bank = psum.tile([P, PIECE], F32, name=f"bank{c}")
-            product(nc, bank[:], gout_q, codes[:], scales[:])
-            nc.scalar.copy(out=c0[:, PIECE * c : PIECE * (c + 1)], in_=bank[:])
+            h, lo = divmod(PIECE * c, BANK)
+            product(nc, c0_banks[h][:, lo : lo + PIECE], gout_q, codes[:], scales[:])
 
-        values_piece(0)
+        t1, s = slots("t1"), slots("s")
+        nc.vector.tensor_copy(t1[:], ta[:].indirect(list1[:]))
+        nc.gpsimd.tensor_tensor(s[:], b1[:], b2[:], ALU.mult)
         values_piece(1)
-        nc.vector.reciprocal(rz[:], z[:])
-        x1, x2, xs = slots("x1"), slots("x2"), slots("xs")
-        nc.vector.tensor_tensor(x1[:], t1[:], b2[:], ALU.mult)
+        values_piece(0)
+        neg_max, z, rz = column("neg_max"), column("z"), column("rz")
+        nc.vector.tensor_reduce(neg_max[:], s[:], AX.X, ALU.max, negate=True)
         values_piece(2)
-        nc.vector.tensor_tensor(x2[:], t2[:], b1[:], ALU.mult)
         values_piece(3)
+        t2, x1 = slots_at("t2", 12 * KB), slots_at("x1", 10 * KB)
+        nc.vector.tensor_copy(t2[:], ta[:].indirect(list2[:]))
+        nc.gpsimd.tensor_tensor(x1[:], t1[:], b2[:], ALU.mult)
+        p = slots_at("p", 0)
+        nc.scalar.activation(out=p[:], in_=s[:], func=ACT.Exp, bias=neg_max[:], scale=1.0, accum_out=z[:])
+        c0 = reuse.tile([P, T], F32, offset=2 * KB)
+        nc.scalar.copy(out=c0[:, :BANK], in_=c0_banks[0][:])
+        nc.scalar.copy(out=c0[:, BANK:], in_=c0_banks[1][:])
+        nc.vector.reciprocal(rz[:], z[:])
+        pn, w, x2, xs = slots("pn"), slots("w"), slots("x2"), slots("xs")
         nc.scalar.activation(out=pn[:], in_=p[:], func=ACT.Copy, scale=rz[:])
-        nc.vector.tensor_tensor(xs[:], x1[:], x2[:], ALU.add)
+        nc.gpsimd.tensor_tensor(x2[:], t2[:], b1[:], ALU.mult)
 
         blocks = BANK // P
         turned = [psum.tile([P, BANK], F32, name=f"turned{h}") for h in range(T // BANK)]
@@ -160,14 +171,15 @@ def tile_attend_hvproductpairs_heads_kernel(tc, query, keys_words, keys_scales, 
         nc.vector.tensor_scalar(w[:], c0[:].indirect(list1[:]), 512.0, 0.0, ALU.mult, ALU.add)
         u, m, c = column("u"), column("m"), column("c")
         xp, wp, ds, r, nx = slots("xp"), slots("wp"), slots("ds"), slots("r"), slots("nx")
-        nc.vector.scalar_tensor_tensor(xp[:], xs[:], rz[:], p[:], ALU.mult, ALU.mult, accum_out=u[:])
-        nc.vector.scalar_tensor_tensor(wp[:], w[:], 1.0, pn[:], ALU.mult, ALU.mult, accum_out=m[:])
-        nc.vector.scalar_tensor_tensor(ds[:], w[:], m[:], pn[:], ALU.subtract, ALU.mult)
-        nc.vector.scalar_tensor_tensor(r[:], xs[:], u[:], ds[:], ALU.subtract, ALU.mult, accum_out=c[:])
         g1, g2, f1, f2 = slots("g1"), slots("g2"), slots("f1"), slots("f2")
+        nc.vector.scalar_tensor_tensor(wp[:], w[:], 1.0, pn[:], ALU.mult, ALU.mult, accum_out=m[:])
+        nc.vector.tensor_tensor(xs[:], x1[:], x2[:], ALU.add)
+        nc.vector.scalar_tensor_tensor(ds[:], w[:], m[:], pn[:], ALU.subtract, ALU.mult)
+        nc.vector.scalar_tensor_tensor(xp[:], xs[:], 1.0, pn[:], ALU.mult, ALU.mult, accum_out=u[:])
         nc.vector.tensor_tensor(g1[:], t2[:], ds[:], ALU.mult)
-        nc.vector.scalar_tensor_tensor(nx[:], pn[:], c[:], r[:], ALU.mult, ALU.subtract)
+        nc.vector.scalar_tensor_tensor(r[:], xs[:], u[:], ds[:], ALU.subtract, ALU.mult, accum_out=c[:])
         nc.vector.tensor_tensor(g2[:], t1[:], ds[:], ALU.mult)
+        nc.vector.scalar_tensor_tensor(nx[:], pn[:], c[:], r[:], ALU.mult, ALU.subtract)
         nc.vector.scalar_tensor_tensor(f1[:], nx[:], -1.0, b2[:], ALU.mult, ALU.mult)
         nc.vector.scalar_tensor_tensor(f2[:], nx[:], -1.0, b1[:], ALU.mult, ALU.mult)
         nc.vector.tensor_tensor(placed1[:].indirect(list1[:]), f1[:], g1[:], ALU.add)

@@ -122,39 +122,45 @@ def tile_attend_hvproductpairs_heads_kernel(tc, query, keys_words, keys_scales, 
         nc.gpsimd.tensor_scalar(first_bf[:], vals_raw[0][:].rearrange("p j w -> p w j"), 1.0, 0.0, ALU.mult, ALU.add)
         vals_bf = [
             first_bf,
-            interleave(nc.scalar.copy, sb, vals_raw[1], PIECE, "vals_bf1"),
+            interleave(nc.scalar.copy, reuse, vals_raw[1], PIECE, "vals_bf1", 7 * KB),
             interleave(nc.scalar.copy, sb, vals_raw[2], PIECE, "vals_bf2"),
-            interleave(nc.scalar.copy, reuse, vals_raw[3], PIECE, "vals_bf3", 11 * KB),
+            interleave(nc.scalar.copy, sb, vals_raw[3], PIECE, "vals_bf3"),
         ]
         gout_q = quantize(nc, sb, gout_bf, Q, "gout")
-        c0_banks = [psum.tile([P, BANK], F32, name=f"bank{h}") for h in range(T // BANK)]
+        c0_first = psum.tile([P, BANK], F32, name="bank0")
+        c0_parts = [c0_first[:, :PIECE], c0_first[:, PIECE:],
+                    psum.tile([P, PIECE], F32, name="bank1")[:], psum.tile([P, PIECE], F32, name="bank2")[:]]
 
         def values_piece(c):
             codes, scales = quantize(nc, sb, vals_bf[c], PIECE, f"vals{c}")
-            h, lo = divmod(PIECE * c, BANK)
-            product(nc, c0_banks[h][:, lo : lo + PIECE], gout_q, codes[:], scales[:])
+            product(nc, c0_parts[c], gout_q, codes[:], scales[:])
 
         t1, s = slots("t1"), slots("s")
         nc.vector.tensor_copy(t1[:], ta[:].indirect(list1[:]))
         nc.gpsimd.tensor_tensor(s[:], b1[:], b2[:], ALU.mult)
-        values_piece(1)
         values_piece(0)
+        values_piece(1)
         neg_max, z, rz = column("neg_max"), column("z"), column("rz")
         nc.vector.tensor_reduce(neg_max[:], s[:], AX.X, ALU.max, negate=True)
-        values_piece(2)
-        values_piece(3)
-        t2, x1 = slots_at("t2", 12 * KB), slots_at("x1", 10 * KB)
+        t2, x1 = slots_at("t2", 8 * KB), slots_at("x1", 6 * KB)
         nc.vector.tensor_copy(t2[:], ta[:].indirect(list2[:]))
         nc.gpsimd.tensor_tensor(x1[:], t1[:], b2[:], ALU.mult)
+        values_piece(2)
+        values_piece(3)
         p = slots_at("p", 0)
         nc.scalar.activation(out=p[:], in_=s[:], func=ACT.Exp, bias=neg_max[:], scale=1.0, accum_out=z[:])
         c0 = reuse.tile([P, T], F32, offset=2 * KB)
-        nc.scalar.copy(out=c0[:, :BANK], in_=c0_banks[0][:])
-        nc.scalar.copy(out=c0[:, BANK:], in_=c0_banks[1][:])
+        nc.scalar.copy(out=c0[:, :BANK], in_=c0_first[:])
+        for c in (2, 3):
+            nc.scalar.copy(out=c0[:, PIECE * c : PIECE * (c + 1)], in_=c0_parts[c])
         nc.vector.reciprocal(rz[:], z[:])
-        pn, w, x2, xs = slots("pn"), slots("w"), slots("x2"), slots("xs")
+        pn, x2, xs = slots("pn"), slots("x2", "vals_bf3"), slots("xs")
+        nc.vector.tensor_tensor(x2[:], t2[:], b1[:], ALU.mult)
+        nc.vector.tensor_tensor(xs[:], x1[:], x2[:], ALU.add)
+        gain, neg_gain = column("gain"), column("neg_gain")
+        nc.scalar.activation(out=gain[:], in_=rz[:], func=ACT.Copy, scale=512.0)
+        nc.scalar.activation(out=neg_gain[:], in_=rz[:], func=ACT.Copy, scale=-512.0)
         nc.scalar.activation(out=pn[:], in_=p[:], func=ACT.Copy, scale=rz[:])
-        nc.gpsimd.tensor_tensor(x2[:], t2[:], b1[:], ALU.mult)
 
         blocks = BANK // P
         turned = [psum.tile([P, BANK], F32, name=f"turned{h}") for h in range(T // BANK)]
@@ -168,20 +174,20 @@ def tile_attend_hvproductpairs_heads_kernel(tc, query, keys_words, keys_scales, 
 
         turn_add(base_sb, True, False)
 
-        nc.vector.tensor_scalar(w[:], c0[:].indirect(list1[:]), 512.0, 0.0, ALU.mult, ALU.add)
-        u, m, c = column("u"), column("m"), column("c")
-        xp, wp, ds, r, nx = slots("xp"), slots("wp"), slots("ds"), slots("r"), slots("nx")
+        u, m, cn = column("u"), column("m"), column("cn")
+        wp, wpn, nd, rn, xds = slots("wp"), slots("wpn"), slots("nd"), slots("rn"), slots("xds")
         g1, g2, f1, f2 = slots("g1"), slots("g2"), slots("f1"), slots("f2")
-        nc.vector.scalar_tensor_tensor(wp[:], w[:], 1.0, pn[:], ALU.mult, ALU.mult, accum_out=m[:])
-        nc.vector.tensor_tensor(xs[:], x1[:], x2[:], ALU.add)
-        nc.vector.scalar_tensor_tensor(ds[:], w[:], m[:], pn[:], ALU.subtract, ALU.mult)
-        nc.vector.scalar_tensor_tensor(xp[:], xs[:], 1.0, pn[:], ALU.mult, ALU.mult, accum_out=u[:])
-        nc.vector.tensor_tensor(g1[:], t2[:], ds[:], ALU.mult)
-        nc.vector.scalar_tensor_tensor(r[:], xs[:], u[:], ds[:], ALU.subtract, ALU.mult, accum_out=c[:])
-        nc.vector.tensor_tensor(g2[:], t1[:], ds[:], ALU.mult)
-        nc.vector.scalar_tensor_tensor(nx[:], pn[:], c[:], r[:], ALU.mult, ALU.subtract)
-        nc.vector.scalar_tensor_tensor(f1[:], nx[:], -1.0, b2[:], ALU.mult, ALU.mult)
-        nc.vector.scalar_tensor_tensor(f2[:], nx[:], -1.0, b1[:], ALU.mult, ALU.mult)
+        nc.vector.tensor_tensor(wp[:], c0[:].indirect(list1[:]), p[:], ALU.mult)
+        nc.scalar.activation(out=wpn[:], in_=wp[:], func=ACT.Copy, scale=rz[:], accum_out=m[:])
+        xp = slots_at("xp", 2 * KB)
+        nc.vector.scalar_tensor_tensor(xp[:], xs[:], rz[:], p[:], ALU.mult, ALU.mult, accum_out=u[:])
+        nc.vector.scalar_tensor_tensor(nd[:], p[:], m[:], wp[:], ALU.mult, ALU.subtract)
+        nc.vector.scalar_tensor_tensor(rn[:], xs[:], u[:], nd[:], ALU.subtract, ALU.mult, accum_out=cn[:])
+        nc.vector.scalar_tensor_tensor(g1[:], t2[:], neg_gain[:], nd[:], ALU.mult, ALU.mult)
+        nc.vector.scalar_tensor_tensor(xds[:], pn[:], cn[:], rn[:], ALU.mult, ALU.subtract)
+        nc.vector.scalar_tensor_tensor(g2[:], t1[:], neg_gain[:], nd[:], ALU.mult, ALU.mult)
+        nc.vector.scalar_tensor_tensor(f1[:], xds[:], gain[:], b2[:], ALU.mult, ALU.mult)
+        nc.vector.scalar_tensor_tensor(f2[:], xds[:], gain[:], b1[:], ALU.mult, ALU.mult)
         nc.vector.tensor_tensor(placed1[:].indirect(list1[:]), f1[:], g1[:], ALU.add)
         nc.vector.tensor_tensor(placed2[:].indirect(list2[:]), f2[:], g2[:], ALU.add)
 

from contextlib import ExitStack

import concourse.mybir as mybir
from concourse.masks import make_identity

D, E, T, Q, I = 512, 512, 1024, 128, 512
FLOPS = 2 * Q * T * (2 * D + E)

F32 = mybir.dt.float32
BF16 = mybir.dt.bfloat16
I32 = mybir.dt.int32
U32 = mybir.dt.uint32
U16 = mybir.dt.uint16
U8 = mybir.dt.uint8
FP8X4 = mybir.dt.float8_e4m3fn_x4
ALU = mybir.AluOpType
ACT = mybir.ActivationFunctionType
AX = mybir.AxisListType

P = 128
PACK = 4
BANK = 512
PIECE = 256


def interleave(copy, pool, raw, width, name, offset=None):
    grouped = pool.tile([P, width, PACK], BF16, align_bytes=64, name=name, offset=offset)
    copy(out=grouped[:].rearrange("p (c i) j -> p c j i", i=4), in_=raw[:].rearrange("p j (c i) -> p c j i", i=4))
    return grouped


def quantize(nc, pool, grouped, width, name):
    codes = pool.tile([P, width], U32, align_bytes=64, name=name + "_codes")
    scales = pool.tile([P, width], U8, align_bytes=64, name=name + "_scales")
    nc.vector.quantize_mx(out=codes[:].bitcast(FP8X4), scales=scales[:], in_=grouped[:].rearrange("p w j -> p (w j)"))
    return codes, scales


def product(nc, bank, rows, codes, scales):
    nc.tensor.matmul_mx(out=bank, lhsT=rows[0][:].bitcast(FP8X4), lhsT_scale=rows[1][:],
                        rhs=codes.bitcast(FP8X4), rhs_scale=scales, start=True, stop=True)


def tile_attend_hvproductpairs_heads_kernel(tc, query, keys_words, keys_scales, gout, vals, dquery, base, offs, offs2, out):
    nc = tc.nc
    with ExitStack() as ctx:
        lists = ctx.enter_context(tc.tile_pool(name="lists", bufs=1))
        sb = ctx.enter_context(tc.tile_pool(name="sb", bufs=1))
        reuse = ctx.enter_context(tc.tile_pool(name="reuse", bufs=1))
        psum = ctx.enter_context(tc.psum_pool(name="psum", bufs=1))

        def load_rows(src, width, name, pool=sb, offset=None):
            raw = pool.tile([P, PACK, width], F32, name=name, offset=offset)
            nc.sync.dma_start(out=raw[:], in_=src.rearrange("(p j) w -> p j w", j=PACK))
            return raw

        key_scales = sb.tile([P, T], U8, align_bytes=64)
        zero = sb.tile([P, 1], F32)
        nc.vector.memset(zero[:], 0.0)
        placed1 = sb.tile([P, T], F32)
        placed2 = sb.tile([P, T], F32)
        nc.vector.memset(placed1[:], 0.0)
        nc.vector.memset(placed2[:], 0.0)

        query_raw = load_rows(query, Q, "query_raw")
        for quad in range(4):
            nc.scalar.dma_start(out=key_scales[32 * quad : 32 * quad + 4, :].bitcast(I32),
                                in_=keys_scales[0, 4 * quad : 4 * quad + 4, :].bitcast(I32))
        key_bytes = keys_words[0].rearrange("p n r -> p (n r)")
        key_words = []
        for h in range(T // BANK):
            words = sb.tile([P, BANK], U32, align_bytes=64, name=f"key_words{h}")
            nc.sync.dma_start(out=words[:].bitcast(I32), in_=key_bytes[:, PACK * BANK * h : PACK * BANK * (h + 1)].bitcast(I32))
            key_words.append(words)
        dquery_raw = load_rows(dquery, Q, "dquery_raw")
        list1 = lists.tile([P, I // 16], U16)
        list2 = lists.tile([P, I // 16], U16)
        nc.sync.dma_start(list1[:], offs)
        nc.sync.dma_start(list2[:], offs2)
        gout_raw = load_rows(gout, Q, "gout_raw")
        vals_raw = [load_rows(vals[:, PIECE * c : PIECE * (c + 1)], PIECE, f"vals_raw{c}") for c in range(T // PIECE - 1)]
        vals_raw.append(load_rows(vals[:, T - PIECE :], PIECE, "vals_raw3", reuse, 0))
        base_sb = sb.tile([P, T], F32)
        nc.sync.dma_start(out=base_sb[:], in_=base)

        warm = sb.tile([P, 1], F32)
        nc.scalar.activation(out=warm[:], in_=zero[:], func=ACT.Exp)
        identity = sb.tile([P, P], F32)
        make_identity(nc, identity[:])

        query_q = quantize(nc, sb, interleave(nc.vector.tensor_copy, sb, query_raw, Q, "query_bf"), Q, "query")
        a = sb.tile([P, T], F32)
        for c in range(T // PIECE):
            bank = psum.tile([P, PIECE], F32, name=f"bank{c}")
            h, lo = divmod(PIECE * c, BANK)
            product(nc, bank[:], query_q, key_words[h][:, lo : lo + PIECE], key_scales[:, PIECE * c : PIECE * (c + 1)])
            nc.vector.tensor_copy(out=a[:, PIECE * c : PIECE * (c + 1)], in_=bank[:])

        dquery_q = quantize(nc, sb, interleave(nc.scalar.copy, sb, dquery_raw, Q, "dquery_bf"), Q, "dquery")
        ta = sb.tile([P, T], F32)
        for h in range(T // BANK):
            bank = psum.tile([P, BANK], F32, name=f"wide{h}")
            product(nc, bank[:], dquery_q, key_words[h][:], key_scales[:, BANK * h : BANK * (h + 1)])
            nc.scalar.copy(out=ta[:, BANK * h : BANK * (h + 1)], in_=bank[:])

        def slots(name, tag=""):
            return sb.tile([P, I], F32, name=name, tag=tag, align_bytes=64)

        def column(name):
            return sb.tile([P, 1], F32, name=name)

        b1, b2 = slots("b1"), slots("b2")
        nc.vector.tensor_scalar(b1[:], a[:].indirect(list1[:]), 1.0, 0.5, ALU.mult, ALU.add)
        nc.vector.tensor_scalar(b2[:], a[:].indirect(list2[:]), 1.0, 0.5, ALU.mult, ALU.add)

        def slots_at(name, offset):
            return reuse.tile([P, I], F32, name=name, offset=offset)

        KB = 1024
        gout_bf = interleave(nc.scalar.copy, sb, gout_raw, Q, "gout_bf")
        first_bf = sb.tile([P, PIECE, PACK], BF16, align_bytes=64)
        nc.gpsimd.tensor_scalar(first_bf[:], vals_raw[0][:].rearrange("p j w -> p w j"), 1.0, 0.0, ALU.mult, ALU.add)
        vals_bf = [
            first_bf,
            interleave(nc.scalar.copy, reuse, vals_raw[1], PIECE, "vals_bf1", 7 * KB),
            interleave(nc.scalar.copy, sb, vals_raw[2], PIECE, "vals_bf2"),
            interleave(nc.scalar.copy, sb, vals_raw[3], PIECE, "vals_bf3"),
        ]
        gout_q = quantize(nc, sb, gout_bf, Q, "gout")
        c0_first = psum.tile([P, BANK], F32, name="bank0")
        c0_parts = [c0_first[:, :PIECE], c0_first[:, PIECE:],
                    psum.tile([P, PIECE], F32, name="bank1")[:], psum.tile([P, PIECE], F32, name="bank2")[:]]

        def values_piece(c):
            codes, scales = quantize(nc, sb, vals_bf[c], PIECE, f"vals{c}")
            product(nc, c0_parts[c], gout_q, codes[:], scales[:])

        t1, s = slots("t1"), slots("s")
        nc.vector.tensor_copy(t1[:], ta[:].indirect(list1[:]))
        nc.gpsimd.tensor_tensor(s[:], b1[:], b2[:], ALU.mult)
        values_piece(0)
        values_piece(1)
        neg_max, z, rz = column("neg_max"), column("z"), column("rz")
        nc.vector.tensor_reduce(neg_max[:], s[:], AX.X, ALU.max, negate=True)
        t2, x1 = slots_at("t2", 8 * KB), slots_at("x1", 6 * KB)
        nc.vector.tensor_copy(t2[:], ta[:].indirect(list2[:]))
        nc.gpsimd.tensor_tensor(x1[:], t1[:], b2[:], ALU.mult)
        values_piece(2)
        values_piece(3)
        p = slots_at("p", 0)
        nc.scalar.activation(out=p[:], in_=s[:], func=ACT.Exp, bias=neg_max[:], scale=1.0, accum_out=z[:])
        c0 = reuse.tile([P, T], F32, offset=2 * KB)
        nc.scalar.copy(out=c0[:, :BANK], in_=c0_first[:])
        for c in (2, 3):
            nc.scalar.copy(out=c0[:, PIECE * c : PIECE * (c + 1)], in_=c0_parts[c])
        nc.vector.reciprocal(rz[:], z[:])
        pn, x2, xs = slots("pn"), slots("x2", "vals_bf3"), slots("xs")
        nc.vector.tensor_tensor(x2[:], t2[:], b1[:], ALU.mult)
        nc.vector.tensor_tensor(xs[:], x1[:], x2[:], ALU.add)
        gain, neg_gain = column("gain"), column("neg_gain")
        nc.scalar.activation(out=gain[:], in_=rz[:], func=ACT.Copy, scale=512.0)
        nc.scalar.activation(out=neg_gain[:], in_=rz[:], func=ACT.Copy, scale=-512.0)
        nc.scalar.activation(out=pn[:], in_=p[:], func=ACT.Copy, scale=rz[:])

        blocks = BANK // P
        turned = [psum.tile([P, BANK], F32, name=f"turned{h}") for h in range(T // BANK)]

        def turn_add(src, first, last):
            for h in range(T // BANK):
                for b in range(blocks):
                    col = BANK * h + P * b
                    nc.tensor.matmul(turned[h][:, P * b : P * (b + 1)], lhsT=src[:, col : col + P], rhs=identity[:],
                                     is_transpose=True, start=first and b == 0, stop=last and b == blocks - 1)

        turn_add(base_sb, True, False)

        u, m, cn = column("u"), column("m"), column("cn")
        wp, wpn, nd, rn, xds = slots("wp"), slots("wpn"), slots("nd"), slots("rn"), slots("xds")
        g1, g2, f1, f2 = slots("g1"), slots("g2"), slots("f1"), slots("f2")
        nc.vector.tensor_tensor(wp[:], c0[:].indirect(list1[:]), p[:], ALU.mult)
        nc.scalar.activation(out=wpn[:], in_=wp[:], func=ACT.Copy, scale=rz[:], accum_out=m[:])
        xp = slots_at("xp", 2 * KB)
        nc.vector.scalar_tensor_tensor(xp[:], xs[:], rz[:], p[:], ALU.mult, ALU.mult, accum_out=u[:])
        nc.vector.scalar_tensor_tensor(nd[:], p[:], m[:], wp[:], ALU.mult, ALU.subtract)
        nc.vector.scalar_tensor_tensor(rn[:], xs[:], u[:], nd[:], ALU.subtract, ALU.mult, accum_out=cn[:])
        nc.vector.scalar_tensor_tensor(g1[:], t2[:], neg_gain[:], nd[:], ALU.mult, ALU.mult)
        nc.vector.scalar_tensor_tensor(xds[:], pn[:], cn[:], rn[:], ALU.mult, ALU.subtract)
        nc.vector.scalar_tensor_tensor(g2[:], t1[:], neg_gain[:], nd[:], ALU.mult, ALU.mult)
        nc.vector.scalar_tensor_tensor(f1[:], xds[:], gain[:], b2[:], ALU.mult, ALU.mult)
        nc.vector.scalar_tensor_tensor(f2[:], xds[:], gain[:], b1[:], ALU.mult, ALU.mult)
        nc.vector.tensor_tensor(placed1[:].indirect(list1[:]), f1[:], g1[:], ALU.add)
        nc.vector.tensor_tensor(placed2[:].indirect(list2[:]), f2[:], g2[:], ALU.add)

        turn_add(placed1, False, True)
        result = sb.tile([P, T], F32)
        for h in range(T // BANK):
            turned_sb = sb.tile([P, BANK], F32, name=f"turned_sb{h}")
            nc.scalar.copy(out=turned_sb[:], in_=turned[h][:])
            back = psum.tile([P, BANK], F32, name=f"wide{h}")
            for b in range(blocks):
                nc.tensor.transpose(back[:, P * b : P * (b + 1)], turned_sb[:, P * b : P * (b + 1)], identity[:])
            cols = slice(BANK * h, BANK * (h + 1))
            nc.vector.tensor_tensor(result[:, cols], back[:], placed2[:, cols], ALU.add)
            nc.sync.dma_start(out=out[:, cols], in_=result[:, cols])
